import numpy as np
import ml_dtypes


def mxq(x, axis, fmt="e4m3"):
    dtype, down = {"e4m3": (ml_dtypes.float8_e4m3fn, 7), "e5m2": (ml_dtypes.float8_e5m2, 14)}[fmt]
    v = np.moveaxis(np.asarray(x, np.float32).astype(ml_dtypes.bfloat16).astype(np.float64), axis, -1)
    blocks = v.reshape(v.shape[:-1] + (-1, 32))
    amax = np.abs(blocks).max(-1, keepdims=True)
    byte = np.maximum(np.where(amax > 0, np.frexp(amax)[1] - 1 + 127, 0) - down, 1)
    scale = np.exp2(byte - 127.0)
    codes = (blocks / scale).astype(np.float32).astype(dtype).astype(np.float64)
    return np.moveaxis((codes * scale).reshape(v.shape), -1, axis)


WIDE = False


def mx_kscale(k):
    if not WIDE:
        return np.ones(k)
    levels = np.array([10, -10, 5, -5, 0])
    if k % 512:
        return np.exp2(np.random.permutation(np.resize(levels, k // 32))).repeat(32)
    a = np.empty((k // 512, 16))
    for p in range(k // 512):
        a[p, :8] = np.random.permutation(np.resize(levels, 8))
        for g in range(8):
            far = levels[np.abs(levels - a[p, g]) >= 10]
            a[p, g + 8] = far[np.random.randint(len(far))]
    return np.exp2(a.ravel()).repeat(32)


def f64(x):
    return np.asarray(x).astype(np.float64)


def striped(idx):
    return np.tile(idx.reshape(-1, 16).T, (8, 1)).astype(np.uint16)


def unstriped(offs):
    return offs[:16].T.reshape(-1).astype(np.int64)


E2M1 = np.array([0.0, 0.5, 1.0, 1.5, 2.0, 3.0, 4.0, 6.0, -0.0, -0.5, -1.0, -1.5, -2.0, -3.0, -4.0, -6.0])


def pack_weight(w, fmt):
    k, n = w.shape
    w = f64(np.asarray(w, np.float32).astype(ml_dtypes.bfloat16)).reshape(k // 32, 32, n)
    amax = np.abs(w).max(1)
    if fmt == "e4m3":
        byte = np.frexp(amax)[1] - 1 + 127 - 7
    else:
        mant, ex = np.frexp(amax / 6.0)
        byte = np.where(mant > 0.5, ex, ex - 1) + 127
    byte = np.clip(np.where(amax > 0, byte, 1), 1, 254)
    scaled = (w * np.exp2(127.0 - byte)[:, None, :]).reshape(k, n).astype(np.float32)
    by_word = np.ascontiguousarray(scaled.reshape(k // 512, 128, 4, n).transpose(0, 1, 3, 2))
    if fmt == "e4m3":
        words = by_word.astype(ml_dtypes.float8_e4m3fn).view(np.uint8)
    else:
        c = by_word.astype(ml_dtypes.float4_e2m1fn).view(np.uint8) & 0xF
        words = (c[..., 0::2] | (c[..., 1::2] << 4)).reshape(k // 512, 128, 2 * n)
    return np.ascontiguousarray(words), np.ascontiguousarray(byte.astype(np.uint8).reshape(k // 512, 16, n))


def unpack_weight(words, scales, fmt):
    g, _, n = scales.shape
    words = np.ascontiguousarray(words).reshape(g, 128, n, -1)
    if fmt == "e4m3":
        vals = words.view(ml_dtypes.float8_e4m3fn).astype(np.float64)
    else:
        nib = np.empty((g, 128, n, 4), np.uint8)
        nib[..., 0::2] = words & 0xF
        nib[..., 1::2] = words >> 4
        vals = E2M1[nib]
    vals = vals * np.repeat(np.exp2(scales.astype(np.float64) - 127.0), 8, axis=1)[..., None]
    return vals.transpose(0, 1, 3, 2).reshape(g * 512, n)


def relu2(v):
    return np.maximum(v, 0.0) ** 2


K, T, E, C, H, N = 512, 768, 9, 256, 512, 256


def by_expert(wq, xq):
    return np.concatenate([wq[e].T @ xq[:, e * C:(e + 1) * C] for e in range(E)], axis=1)


def setup_inputs():
    n = np.random.standard_normal
    s = mx_kscale(K)
    u = mx_kscale(H)
    slot_token = np.concatenate([np.random.permutation(T)[:C] for e in range(E)])
    partner = np.concatenate([np.random.permutation(T) for _ in range(-(-E * C // T))])[:E * C]
    x = pack_weight(n((K, T)) * s[:, None], "e4m3")
    w1 = [pack_weight(m, "e4m3") for m in n((E, K, H)) / np.sqrt(K) / s[None, :, None] * u]
    wp = [pack_weight(m, "e4m3") for m in n((E, K, H)) / np.sqrt(K) / s[None, :, None] * u]
    w2 = [pack_weight(m, "e4m3") for m in n((E, H, N)) / np.sqrt(H) / u[None, :, None] ** 2]
    return {
        "x_words": x[0],
        "x_scales": x[1],
        "w1_words": np.stack([m[0] for m in w1]),
        "w1_scales": np.stack([m[1] for m in w1]),
        "wp_words": np.stack([m[0] for m in wp]),
        "wp_scales": np.stack([m[1] for m in wp]),
        "w2_words": np.stack([m[0] for m in w2]),
        "w2_scales": np.stack([m[1] for m in w2]),
        "offs": striped(slot_token),
        "offs2": striped(partner),
    }


def reference(x_words, x_scales, w1_words, w1_scales, wp_words, wp_scales, w2_words, w2_scales, offs, offs2):
    w1 = np.stack([unpack_weight(w1_words[e], w1_scales[e], "e4m3") for e in range(E)])
    wp = np.stack([unpack_weight(wp_words[e], wp_scales[e], "e4m3") for e in range(E)])
    w2 = np.stack([unpack_weight(w2_words[e], w2_scales[e], "e4m3") for e in range(E)])
    idx, idx2 = unstriped(offs), unstriped(offs2)
    x = unpack_weight(x_words, x_scales, "e4m3")
    h = relu2(by_expert(w1, x[:, idx]) + by_expert(wp, x[:, idx2]))
    y = by_expert(w2, mxq(h, 0, "e4m3"))
    out = y
    return out

@@ -1,0 +1,189 @@
+from contextlib import ExitStack
+
+import concourse.mybir as mybir
+from concourse.masks import make_identity
+
+K, T, E, C, H, N = 512, 768, 9, 256, 512, 256
+FLOPS = 2 * E * C * (2 * K * H + H * N)
+
+F32 = mybir.dt.float32
+BF16 = mybir.dt.bfloat16
+I32 = mybir.dt.int32
+U32 = mybir.dt.uint32
+U16 = mybir.dt.uint16
+U8 = mybir.dt.uint8
+FP8X4 = mybir.dt.float8_e4m3fn_x4
+ACT = mybir.ActivationFunctionType
+
+P = 128
+PACK = 4
+BLOCKS = C // P
+LIST_COLS = C // 16
+LAG = 3
+VECTOR_OUT = range(4, 8)
+W1_ROW, WP_ROW, W2_ROW = 4, 8, 12
+LOAD_GROUPS = ((0, 1), (1, 2), (2, 4), (4, 6), (6, 9))
+
+
+def tile_moe_duo_s_relu2_kernel(
+    tc, x_words, x_scales, w1_words, w1_scales, wp_words, wp_scales, w2_words, w2_scales, offs, offs2, out
+):
+    nc = tc.nc
+    with ExitStack() as ctx:
+        keep = ctx.enter_context(tc.tile_pool(name="keep", bufs=1))
+        work = ctx.enter_context(tc.tile_pool(name="work", bufs=3))
+        psum = ctx.enter_context(tc.psum_pool(name="psum", bufs=1))
+
+        tok_list = keep.tile([P, E * LIST_COLS], U16, name="tok_list")
+        par_list = keep.tile([P, E * LIST_COLS], U16, name="par_list")
+        x_codes = keep.tile([P, T], U32, name="x_codes", align_bytes=64)
+        x_plane = keep.tile([P, T], U8, name="x_plane", align_bytes=64)
+        w_plane = keep.tile([P, E * H], U8, name="w_plane", align_bytes=64)
+        w2_plane = keep.tile([P, E * N], U8, name="w2_plane", align_bytes=64)
+        ident = keep.tile([P, P], F32, name="ident")
+
+        for plane in (w_plane, w2_plane):
+            nc.vector.memset(plane[:].bitcast(I32), 0)
+
+        def load_scales(plane, first_row, scales):
+            rows = scales.bitcast(I32).rearrange("e (q r) c -> r q e c", r=4)
+            dst = plane[:].bitcast(I32).rearrange("p (e c) -> p e c", e=rows.shape[2])
+            for r in range(4):
+                nc.sync.dma_start(out=dst[first_row + r : P : 32, :, :], in_=rows[r])
+
+        codes = {}
+
+        def load_words(name, words, group):
+            lo, hi = group
+            width = words.shape[3]
+            held = keep.tile([P, hi - lo, width], U32, name="%s_%d" % (name, lo), align_bytes=64)
+            src = words[lo:hi, 0].rearrange("e p c d -> p e (c d)")
+            nc.sync.dma_start(out=held[:].bitcast(I32), in_=src.bitcast(I32))
+            for e in range(lo, hi):
+                codes[name, e] = held[:, e - lo, :]
+
+        make_identity(nc, ident[:])
+        nc.sync.dma_start(tok_list[:], offs)
+        nc.sync.dma_start(par_list[:], offs2)
+        x_rows = x_scales[0].bitcast(I32).rearrange("(q r) c -> q r c", r=4)
+        for q in range(4):
+            src = x_rows[q].unsqueeze(0).broadcast_to([8, 4, T // 4])
+            nc.sync.dma_start(out=x_plane[:].bitcast(I32)[32 * q : 32 * q + 32, :], in_=src)
+        nc.sync.dma_start(out=x_codes[:].bitcast(I32), in_=x_words[0].rearrange("p t d -> p (t d)").bitcast(I32))
+        load_words("w1", w1_words, LOAD_GROUPS[0])
+        load_scales(w_plane, W1_ROW, w1_scales[:, 0])
+        load_scales(w_plane, WP_ROW, wp_scales[:, 0])
+        load_words("wp", wp_words, LOAD_GROUPS[0])
+        for g, group in enumerate(LOAD_GROUPS[1:]):
+            load_words("w1", w1_words, group)
+            load_words("wp", wp_words, group)
+            if g == 0:
+                load_scales(w2_plane, W2_ROW, w2_scales[:, 0])
+            load_words("w2", w2_words, LOAD_GROUPS[g])
+        load_words("w2", w2_words, LOAD_GROUPS[-1])
+
+        out_rows = out.rearrange("(t p) s -> p t s", p=P)
+        picked, hidden, quantised = {}, {}, {}
+
+        def bank(tag, shape):
+            return psum.tile(shape, F32, name="acc", tag=tag)
+
+        def lane(e, shape, dtype, name):
+            return keep.tile(shape, dtype, name="%s_%d" % (name, e), tag="lane%d" % (e % (LAG + 1)), align_bytes=64)
+
+        def gather(e):
+            cols = slice(e * LIST_COLS, (e + 1) * LIST_COLS)
+            tok_codes = lane(e, [P, C], U32, "tok_codes")
+            par_codes = work.tile([P, C], U32, name="par_codes", align_bytes=64)
+            tok_plane = work.tile([P, C], U8, name="tok_plane", align_bytes=64, bufs=2)
+            par_plane = work.tile([P, C], U8, name="par_plane", align_bytes=64, bufs=2)
+            nc.vector.tensor_copy(tok_plane[:], x_plane[:].indirect(tok_list[:, cols]))
+            nc.vector.tensor_copy(par_plane[:], x_plane[:].indirect(par_list[:, cols]))
+            nc.vector.tensor_copy(tok_codes[:], x_codes[:].indirect(tok_list[:, cols]))
+            nc.vector.tensor_copy(par_codes[:], x_codes[:].indirect(par_list[:, cols]))
+            picked[e] = ((tok_codes, tok_plane, "w1", W1_ROW), (par_codes, par_plane, "wp", WP_ROW))
+
+        def first_layer(e, b):
+            acc = bank("x%d" % ((e - b) % 2), [P, H])
+            slots = slice(b * P, (b + 1) * P)
+            for n, (words, plane, name, row) in enumerate(picked[e]):
+                nc.tensor.matmul_mx(
+                    out=acc[:],
+                    lhsT=words[:, slots].bitcast(FP8X4),
+                    lhsT_scale=plane[:, slots],
+                    rhs=codes[name, e].bitcast(FP8X4),
+                    rhs_scale=w_plane[row:P, e * H : (e + 1) * H],
+                    start=(n == 0),
+                    stop=(n == 1),
+                )
+            return acc
+
+        def relu(acc, on_vector):
+            pos = work.tile([P, PACK, P], F32, name="pos")
+            src = acc[:].rearrange("s (m t) -> s t m", t=PACK)
+            if on_vector:
+                nc.vector.tensor_scalar_max(pos[:], src, 0.0)
+            else:
+                nc.scalar.activation(pos[:], src, ACT.Relu)
+            return pos
+
+        def turn(e, b, pos):
+            tag = ("z%d" % b) if e == E - 1 else "%s%d" % ("xy"[b], e % 2)
+            turned = bank(tag, [P, PACK, P])
+            for t in range(PACK):
+                nc.tensor.transpose(turned[:, t, :], pos[:, t, :], ident[:])
+            return turned
+
+        def square(e, b, turned):
+            nc.scalar.activation(
+                hidden[e][:, b * P : (b + 1) * P, :], turned[:].rearrange("p t s -> p s t"), ACT.Square
+            )
+
+        def quantise(e):
+            h_codes = work.tile([P, C], U32, name="h_codes", align_bytes=64)
+            h_plane = work.tile([P, C], U8, name="h_plane", align_bytes=64)
+            nc.vector.quantize_mx(
+                out=h_codes[:].bitcast(FP8X4), scales=h_plane[:], in_=hidden[e][:].rearrange("p s t -> p (s t)")
+            )
+            quantised[e] = (h_codes, h_plane)
+
+        def second_layer(step, e, on_vector):
+            h_codes, h_plane = quantised[e]
+            if step < E:
+                tag = "y%d" % ((step - 1) % 2)
+            elif e == E - 1:
+                tag = "z2"
+            else:
+                tag = "x%d" % (e % 2)
+            acc = bank(tag, [P, N // P, C])
+            for t in range(N // P):
+                nc.tensor.matmul_mx(
+                    out=acc[:, t, :],
+                    lhsT=codes["w2", e][:, t * P : (t + 1) * P].bitcast(FP8X4),
+                    lhsT_scale=w2_plane[W2_ROW:P, e * N + t * P : e * N + (t + 1) * P],
+                    rhs=h_codes[:].bitcast(FP8X4),
+                    rhs_scale=h_plane[:],
+                    start=True,
+                    stop=True,
+                )
+            y = work.tile([P, N // P, C], F32, name="y")
+            if on_vector:
+                nc.vector.tensor_copy(y[:], acc[:])
+            else:
+                nc.scalar.copy(y[:], acc[:])
+            nc.sync.dma_start(out=out_rows[:, :, e * C : (e + 1) * C], in_=y[:])
+
+        for step in range(E + LAG):
+            if step < E:
+                gather(step)
+            if step >= LAG:
+                quantise(step - LAG)
+            if step < E:
+                accs = [first_layer(step, b) for b in range(BLOCKS)]
+                rectified = [relu(accs[b], step == E - 1 and b == 1) for b in range(BLOCKS)]
+            if step >= LAG:
+                second_layer(step, step - LAG, step - LAG in VECTOR_OUT)
+            if step < E:
+                hidden[step] = lane(step, [P, C, PACK], BF16, "hidden")
+                for b in range(BLOCKS):
+                    square(step, b, turn(step, b, rectified[b]))

@@ -17,12 +17,20 @@ ACT = mybir.ActivationFunctionType
 
 P = 128
 PACK = 4
+QUADS = 4
 BLOCKS = C // P
-LIST_COLS = C // 16
-LAG = 3
-VECTOR_OUT = range(4, 8)
+LAST = E - 1
+BLOCK_COLS = P // 16
+
+FRONT = 4
 W1_ROW, WP_ROW, W2_ROW = 4, 8, 12
-LOAD_GROUPS = ((0, 1), (1, 2), (2, 4), (4, 6), (6, 9))
+FRONT_GROUPS = ((0, 1), (1, 2), (2, FRONT))
+REST_GROUPS = ((FRONT, 6), (6, E))
+W2_GROUPS = ((0, 2), (2, 4), (4, 6), (6, E))
+BYTE_BLOCKS = 3
+AHEAD = 2
+LAG = 3
+VECTOR_OUT = range(LAG, LAST - 1)
 
 
 def tile_moe_duo_s_relu2_kernel(
@@ -34,16 +42,23 @@ def tile_moe_duo_s_relu2_kernel(
         work = ctx.enter_context(tc.tile_pool(name="work", bufs=3))
         psum = ctx.enter_context(tc.psum_pool(name="psum", bufs=1))
 
-        tok_list = keep.tile([P, E * LIST_COLS], U16, name="tok_list")
-        par_list = keep.tile([P, E * LIST_COLS], U16, name="par_list")
+        tok_list = keep.tile([P, E * BLOCKS * BLOCK_COLS], U16, name="tok_list")
+        par_list = keep.tile([P, E * BLOCKS * BLOCK_COLS], U16, name="par_list")
         x_codes = keep.tile([P, T], U32, name="x_codes", align_bytes=64)
         x_plane = keep.tile([P, T], U8, name="x_plane", align_bytes=64)
-        w_plane = keep.tile([P, E * H], U8, name="w_plane", align_bytes=64)
+        front_plane = keep.tile([P, 2 * H], U8, name="front_plane", align_bytes=64)
+        rest_plane = keep.tile([P, (E - FRONT) * H], U8, name="rest_plane", align_bytes=64)
         w2_plane = keep.tile([P, E * N], U8, name="w2_plane", align_bytes=64)
         ident = keep.tile([P, P], F32, name="ident")
 
-        for plane in (w_plane, w2_plane):
+        for plane in (x_plane, front_plane, w2_plane, rest_plane):
             nc.vector.memset(plane[:].bitcast(I32), 0)
+
+        def load_front_scales(column, scales):
+            dst = front_plane[:, column : column + H].bitcast(I32)
+            for q in range(QUADS):
+                src = scales[:FRONT, 0, 4 * q : 4 * q + 4, :].bitcast(I32)
+                nc.sync.dma_start(out=dst[32 * q : 32 * q + 4 * FRONT, :], in_=src)
 
         def load_scales(plane, first_row, scales):
             rows = scales.bitcast(I32).rearrange("e (q r) c -> r q e c", r=4)
@@ -51,12 +66,18 @@ def tile_moe_duo_s_relu2_kernel(
             for r in range(4):
                 nc.sync.dma_start(out=dst[first_row + r : P : 32, :, :], in_=rows[r])
 
+        def first_scales(name, e):
+            if e < FRONT:
+                column = 0 if name == "w1" else H
+                return front_plane[4 * e : P, column : column + H]
+            first_row = W1_ROW if name == "w1" else WP_ROW
+            return rest_plane[first_row:P, (e - FRONT) * H : (e - FRONT + 1) * H]
+
         codes = {}
 
         def load_words(name, words, group):
             lo, hi = group
-            width = words.shape[3]
-            held = keep.tile([P, hi - lo, width], U32, name="%s_%d" % (name, lo), align_bytes=64)
+            held = keep.tile([P, hi - lo, words.shape[3]], U32, name="%s_%d" % (name, lo), align_bytes=64)
             src = words[lo:hi, 0].rearrange("e p c d -> p e (c d)")
             nc.sync.dma_start(out=held[:].bitcast(I32), in_=src.bitcast(I32))
             for e in range(lo, hi):
@@ -65,61 +86,69 @@ def tile_moe_duo_s_relu2_kernel(
         make_identity(nc, ident[:])
         nc.sync.dma_start(tok_list[:], offs)
         nc.sync.dma_start(par_list[:], offs2)
-        x_rows = x_scales[0].bitcast(I32).rearrange("(q r) c -> q r c", r=4)
-        for q in range(4):
-            src = x_rows[q].unsqueeze(0).broadcast_to([8, 4, T // 4])
-            nc.sync.dma_start(out=x_plane[:].bitcast(I32)[32 * q : 32 * q + 32, :], in_=src)
+        for q in range(QUADS):
+            src = x_scales[0, 4 * q : 4 * q + 4, :].bitcast(I32)
+            nc.sync.dma_start(out=x_plane[:].bitcast(I32)[32 * q : 32 * q + 4, :], in_=src)
         nc.sync.dma_start(out=x_codes[:].bitcast(I32), in_=x_words[0].rearrange("p t d -> p (t d)").bitcast(I32))
-        load_words("w1", w1_words, LOAD_GROUPS[0])
-        load_scales(w_plane, W1_ROW, w1_scales[:, 0])
-        load_scales(w_plane, WP_ROW, wp_scales[:, 0])
-        load_words("wp", wp_words, LOAD_GROUPS[0])
-        for g, group in enumerate(LOAD_GROUPS[1:]):
+        load_words("w1", w1_words, FRONT_GROUPS[0])
+        load_front_scales(0, w1_scales)
+        load_front_scales(H, wp_scales)
+        load_words("wp", wp_words, FRONT_GROUPS[0])
+        for group in FRONT_GROUPS[1:]:
             load_words("w1", w1_words, group)
             load_words("wp", wp_words, group)
-            if g == 0:
-                load_scales(w2_plane, W2_ROW, w2_scales[:, 0])
-            load_words("w2", w2_words, LOAD_GROUPS[g])
-        load_words("w2", w2_words, LOAD_GROUPS[-1])
+        load_scales(w2_plane, W2_ROW, w2_scales[:, 0])
+        load_scales(rest_plane, W1_ROW, w1_scales[FRONT:, 0])
+        load_scales(rest_plane, WP_ROW, wp_scales[FRONT:, 0])
+        for w2_group, group in zip(W2_GROUPS, REST_GROUPS):
+            load_words("w2", w2_words, w2_group)
+            load_words("w1", w1_words, group)
+            load_words("wp", wp_words, group)
+        for w2_group in W2_GROUPS[len(REST_GROUPS) :]:
+            load_words("w2", w2_words, w2_group)
 
-        out_rows = out.rearrange("(t p) s -> p t s", p=P)
-        picked, hidden, quantised = {}, {}, {}
+        out_rows = out.rearrange("(u p) s -> p u s", p=P)
+        lists = {"w1": tok_list, "wp": par_list}
+        picked_codes, picked_plane, hidden = {}, {}, {}
 
         def bank(tag, shape):
             return psum.tile(shape, F32, name="acc", tag=tag)
 
-        def lane(e, shape, dtype, name):
-            return keep.tile(shape, dtype, name="%s_%d" % (name, e), tag="lane%d" % (e % (LAG + 1)), align_bytes=64)
+        def gather_into(picked, name, held, window, first, count):
+            cols = slice(first * BLOCK_COLS, (first + count) * BLOCK_COLS)
+            nc.vector.tensor_copy(held[:], window[:].indirect(lists[name][:, cols]))
+            for j in range(count):
+                picked[name, first + j] = held[:, j * P : (j + 1) * P]
 
-        def gather(e):
-            cols = slice(e * LIST_COLS, (e + 1) * LIST_COLS)
-            tok_codes = lane(e, [P, C], U32, "tok_codes")
-            par_codes = work.tile([P, C], U32, name="par_codes", align_bytes=64)
-            tok_plane = work.tile([P, C], U8, name="tok_plane", align_bytes=64, bufs=2)
-            par_plane = work.tile([P, C], U8, name="par_plane", align_bytes=64, bufs=2)
-            nc.vector.tensor_copy(tok_plane[:], x_plane[:].indirect(tok_list[:, cols]))
-            nc.vector.tensor_copy(par_plane[:], x_plane[:].indirect(par_list[:, cols]))
-            nc.vector.tensor_copy(tok_codes[:], x_codes[:].indirect(tok_list[:, cols]))
-            nc.vector.tensor_copy(par_codes[:], x_codes[:].indirect(par_list[:, cols]))
-            picked[e] = ((tok_codes, tok_plane, "w1", W1_ROW), (par_codes, par_plane, "wp", WP_ROW))
+        def gather(block):
+            for name in ("w1", "wp"):
+                if (name, block) not in picked_plane:
+                    held = work.tile([P, BYTE_BLOCKS * P], U8, name="slot_plane_" + name, align_bytes=64, bufs=AHEAD)
+                    gather_into(picked_plane, name, held, x_plane, block, BYTE_BLOCKS)
+            count = 1 if block // BLOCKS == LAST else BLOCKS
+            for name in ("w1", "wp"):
+                if (name, block) not in picked_codes:
+                    held = work.tile([P, count * P], U32, name="slot_codes_" + name, align_bytes=64, bufs=AHEAD)
+                    gather_into(picked_codes, name, held, x_codes, block, count)
 
         def first_layer(e, b):
-            acc = bank("x%d" % ((e - b) % 2), [P, H])
-            slots = slice(b * P, (b + 1) * P)
-            for n, (words, plane, name, row) in enumerate(picked[e]):
+            block = e * BLOCKS + b
+            gather(block)
+            acc = bank("a%d" % b, [P, H])
+            for name in ("w1", "wp"):
                 nc.tensor.matmul_mx(
                     out=acc[:],
-                    lhsT=words[:, slots].bitcast(FP8X4),
-                    lhsT_scale=plane[:, slots],
+                    lhsT=picked_codes[name, block].bitcast(FP8X4),
+                    lhsT_scale=picked_plane[name, block],
                     rhs=codes[name, e].bitcast(FP8X4),
-                    rhs_scale=w_plane[row:P, e * H : (e + 1) * H],
-                    start=(n == 0),
-                    stop=(n == 1),
+                    rhs_scale=first_scales(name, e),
+                    start=(name == "w1"),
+                    stop=(name == "wp"),
                 )
             return acc
 
         def relu(acc, on_vector):
-            pos = work.tile([P, PACK, P], F32, name="pos")
+            pos = work.tile([P, PACK, P], F32, name="pos", bufs=2 * BLOCKS)
             src = acc[:].rearrange("s (m t) -> s t m", t=PACK)
             if on_vector:
                 nc.vector.tensor_scalar_max(pos[:], src, 0.0)
@@ -128,62 +157,77 @@ def tile_moe_duo_s_relu2_kernel(
             return pos
 
         def turn(e, b, pos):
-            tag = ("z%d" % b) if e == E - 1 else "%s%d" % ("xy"[b], e % 2)
-            turned = bank(tag, [P, PACK, P])
+            turned = bank("%s%d" % ("pq"[b], e % (2 + b)), [P, PACK, P])
             for t in range(PACK):
                 nc.tensor.transpose(turned[:, t, :], pos[:, t, :], ident[:])
             return turned
 
-        def square(e, b, turned):
-            nc.scalar.activation(
-                hidden[e][:, b * P : (b + 1) * P, :], turned[:].rearrange("p t s -> p s t"), ACT.Square
-            )
+        def squares(e, turned):
+            hidden[e] = keep.tile([P, C, PACK], BF16, name="hidden_%d" % e, align_bytes=64)
+            for b in range(BLOCKS):
+                src = turned[b][:].rearrange("m t s -> m s t")
+                nc.scalar.activation(hidden[e][:, b * P : (b + 1) * P, :], src, ACT.Square)
 
-        def quantise(e):
-            h_codes = work.tile([P, C], U32, name="h_codes", align_bytes=64)
-            h_plane = work.tile([P, C], U8, name="h_plane", align_bytes=64)
-            nc.vector.quantize_mx(
-                out=h_codes[:].bitcast(FP8X4), scales=h_plane[:], in_=hidden[e][:].rearrange("p s t -> p (s t)")
-            )
-            quantised[e] = (h_codes, h_plane)
+        def quantise(e, slots):
+            width = slots.stop - slots.start
+            h_codes = work.tile([P, width], U32, name="h_codes", align_bytes=64)
+            h_plane = work.tile([P, width], U8, name="h_plane", align_bytes=64)
+            src = hidden[e][:, slots, :].rearrange("m s t -> m (s t)")
+            nc.vector.quantize_mx(out=h_codes[:].bitcast(FP8X4), scales=h_plane[:], in_=src)
+            return h_codes, h_plane
 
-        def second_layer(step, e, on_vector):
-            h_codes, h_plane = quantised[e]
-            if step < E:
-                tag = "y%d" % ((step - 1) % 2)
-            elif e == E - 1:
-                tag = "z2"
-            else:
-                tag = "x%d" % (e % 2)
-            acc = bank(tag, [P, N // P, C])
-            for t in range(N // P):
+        def second_layer(e, slots, quantised, tag):
+            h_codes, h_plane = quantised
+            acc = bank(tag, [P, N // P, slots.stop - slots.start])
+            for u in range(N // P):
                 nc.tensor.matmul_mx(
-                    out=acc[:, t, :],
-                    lhsT=codes["w2", e][:, t * P : (t + 1) * P].bitcast(FP8X4),
-                    lhsT_scale=w2_plane[W2_ROW:P, e * N + t * P : e * N + (t + 1) * P],
+                    out=acc[:, u, :],
+                    lhsT=codes["w2", e][:, u * P : (u + 1) * P].bitcast(FP8X4),
+                    lhsT_scale=w2_plane[W2_ROW:P, e * N + u * P : e * N + (u + 1) * P],
                     rhs=h_codes[:].bitcast(FP8X4),
                     rhs_scale=h_plane[:],
                     start=True,
                     stop=True,
                 )
-            y = work.tile([P, N // P, C], F32, name="y")
-            if on_vector:
+            return acc
+
+        def leave(e, slots, acc):
+            y = work.tile([P, N // P, slots.stop - slots.start], F32, name="y", bufs=LAST + BLOCKS)
+            if e in VECTOR_OUT:
                 nc.vector.tensor_copy(y[:], acc[:])
             else:
                 nc.scalar.copy(y[:], acc[:])
-            nc.sync.dma_start(out=out_rows[:, :, e * C : (e + 1) * C], in_=y[:])
+            nc.sync.dma_start(out=out_rows[:, :, e * C + slots.start : e * C + slots.stop], in_=y[:])
 
-        for step in range(E + LAG):
-            if step < E:
-                gather(step)
-            if step >= LAG:
-                quantise(step - LAG)
-            if step < E:
-                accs = [first_layer(step, b) for b in range(BLOCKS)]
-                rectified = [relu(accs[b], step == E - 1 and b == 1) for b in range(BLOCKS)]
-            if step >= LAG:
-                second_layer(step, step - LAG, step - LAG in VECTOR_OUT)
-            if step < E:
-                hidden[step] = lane(step, [P, C, PACK], BF16, "hidden")
-                for b in range(BLOCKS):
-                    square(step, b, turn(step, b, rectified[b]))
+        whole = slice(0, C)
+        accs = [first_layer(0, b) for b in range(BLOCKS)]
+        turned = None
+        for e in range(E):
+            behind = e - LAG
+            if behind >= 0:
+                quantised = quantise(behind, whole)
+            if e < LAST:
+                gather((e + 1) * BLOCKS)
+            if behind >= 0:
+                sums = second_layer(behind, whole, quantised, "q%d" % ((e + 1) % 3))
+            if e == LAST:
+                squares(e - 1, turned)
+            rectified = [relu(accs[0], e == LAST)]
+            if e < LAST:
+                accs[0] = first_layer(e + 1, 0)
+            rectified.append(relu(accs[1], False))
+            if behind >= 0:
+                leave(behind, whole, sums)
+            before = turned
+            turned = [turn(e, b, rectified[b]) for b in range(BLOCKS)]
+            if e < LAST:
+                accs[1] = first_layer(e + 1, 1)
+                if e > 0:
+                    squares(e - 1, before)
+
+        for e, tag in zip(range(E - LAG, LAST), ("z", "q%d" % ((LAST - 2) % 3))):
+            leave(e, whole, second_layer(e, whole, quantise(e, whole), tag))
+        squares(LAST, turned)
+        for b in range(BLOCKS):
+            slots = slice(b * P, (b + 1) * P)
+            leave(LAST, slots, second_layer(LAST, slots, quantise(LAST, slots), "a%d" % b))

from contextlib import ExitStack

import concourse.mybir as mybir
from concourse.masks import make_identity

K, T, E, C, H, N = 512, 768, 9, 256, 512, 256
FLOPS = 2 * E * C * (2 * K * H + H * N)

F32 = mybir.dt.float32
BF16 = mybir.dt.bfloat16
I32 = mybir.dt.int32
U32 = mybir.dt.uint32
U16 = mybir.dt.uint16
U8 = mybir.dt.uint8
FP8X4 = mybir.dt.float8_e4m3fn_x4
ACT = mybir.ActivationFunctionType

P = 128
PACK = 4
QUADS = 4
BLOCKS = C // P
LAST = E - 1
BLOCK_COLS = P // 16

FRONT = 4
W1_ROW, WP_ROW, W2_ROW = 4, 8, 12
FRONT_GROUPS = ((0, 1), (1, 2), (2, FRONT))
REST_GROUPS = ((FRONT, 6), (6, E))
W2_GROUPS = ((0, 2), (2, 4), (4, 6), (6, E))
BYTE_BLOCKS = 3
AHEAD = 2
LAG = 3
VECTOR_OUT = range(LAG, LAST - 1)


def tile_moe_duo_s_relu2_kernel(
    tc, x_words, x_scales, w1_words, w1_scales, wp_words, wp_scales, w2_words, w2_scales, offs, offs2, out
):
    nc = tc.nc
    with ExitStack() as ctx:
        keep = ctx.enter_context(tc.tile_pool(name="keep", bufs=1))
        work = ctx.enter_context(tc.tile_pool(name="work", bufs=3))
        psum = ctx.enter_context(tc.psum_pool(name="psum", bufs=1))

        tok_list = keep.tile([P, E * BLOCKS * BLOCK_COLS], U16, name="tok_list")
        par_list = keep.tile([P, E * BLOCKS * BLOCK_COLS], U16, name="par_list")
        x_codes = keep.tile([P, T], U32, name="x_codes", align_bytes=64)
        x_plane = keep.tile([P, T], U8, name="x_plane", align_bytes=64)
        front_plane = keep.tile([P, 2 * H], U8, name="front_plane", align_bytes=64)
        rest_plane = keep.tile([P, (E - FRONT) * H], U8, name="rest_plane", align_bytes=64)
        w2_plane = keep.tile([P, E * N], U8, name="w2_plane", align_bytes=64)
        ident = keep.tile([P, P], F32, name="ident")

        for plane in (x_plane, front_plane, w2_plane, rest_plane):
            nc.vector.memset(plane[:].bitcast(I32), 0)

        def load_front_scales(column, scales):
            dst = front_plane[:, column : column + H].bitcast(I32)
            for q in range(QUADS):
                src = scales[:FRONT, 0, 4 * q : 4 * q + 4, :].bitcast(I32)
                nc.sync.dma_start(out=dst[32 * q : 32 * q + 4 * FRONT, :], in_=src)

        def load_scales(plane, first_row, scales):
            rows = scales.bitcast(I32).rearrange("e (q r) c -> r q e c", r=4)
            dst = plane[:].bitcast(I32).rearrange("p (e c) -> p e c", e=rows.shape[2])
            for r in range(4):
                nc.sync.dma_start(out=dst[first_row + r : P : 32, :, :], in_=rows[r])

        def first_scales(name, e):
            if e < FRONT:
                column = 0 if name == "w1" else H
                return front_plane[4 * e : P, column : column + H]
            first_row = W1_ROW if name == "w1" else WP_ROW
            return rest_plane[first_row:P, (e - FRONT) * H : (e - FRONT + 1) * H]

        codes = {}

        def load_words(name, words, group):
            lo, hi = group
            held = keep.tile([P, hi - lo, words.shape[3]], U32, name="%s_%d" % (name, lo), align_bytes=64)
            src = words[lo:hi, 0].rearrange("e p c d -> p e (c d)")
            nc.sync.dma_start(out=held[:].bitcast(I32), in_=src.bitcast(I32))
            for e in range(lo, hi):
                codes[name, e] = held[:, e - lo, :]

        make_identity(nc, ident[:])
        nc.sync.dma_start(tok_list[:], offs)
        nc.sync.dma_start(par_list[:], offs2)
        for q in range(QUADS):
            src = x_scales[0, 4 * q : 4 * q + 4, :].bitcast(I32)
            nc.sync.dma_start(out=x_plane[:].bitcast(I32)[32 * q : 32 * q + 4, :], in_=src)
        nc.sync.dma_start(out=x_codes[:].bitcast(I32), in_=x_words[0].rearrange("p t d -> p (t d)").bitcast(I32))
        load_words("w1", w1_words, FRONT_GROUPS[0])
        load_front_scales(0, w1_scales)
        load_front_scales(H, wp_scales)
        load_words("wp", wp_words, FRONT_GROUPS[0])
        for group in FRONT_GROUPS[1:]:
            load_words("w1", w1_words, group)
            load_words("wp", wp_words, group)
        load_scales(w2_plane, W2_ROW, w2_scales[:, 0])
        load_scales(rest_plane, W1_ROW, w1_scales[FRONT:, 0])
        load_scales(rest_plane, WP_ROW, wp_scales[FRONT:, 0])
        for w2_group, group in zip(W2_GROUPS, REST_GROUPS):
            load_words("w2", w2_words, w2_group)
            load_words("w1", w1_words, group)
            load_words("wp", wp_words, group)
        for w2_group in W2_GROUPS[len(REST_GROUPS) :]:
            load_words("w2", w2_words, w2_group)

        out_rows = out.rearrange("(u p) s -> p u s", p=P)
        lists = {"w1": tok_list, "wp": par_list}
        picked_codes, picked_plane, hidden = {}, {}, {}

        def bank(tag, shape):
            return psum.tile(shape, F32, name="acc", tag=tag)

        def gather_into(picked, name, held, window, first, count):
            cols = slice(first * BLOCK_COLS, (first + count) * BLOCK_COLS)
            nc.vector.tensor_copy(held[:], window[:].indirect(lists[name][:, cols]))
            for j in range(count):
                picked[name, first + j] = held[:, j * P : (j + 1) * P]

        def gather(block):
            for name in ("w1", "wp"):
                if (name, block) not in picked_plane:
                    held = work.tile([P, BYTE_BLOCKS * P], U8, name="slot_plane_" + name, align_bytes=64, bufs=AHEAD)
                    gather_into(picked_plane, name, held, x_plane, block, BYTE_BLOCKS)
            count = 1 if block // BLOCKS == LAST else BLOCKS
            for name in ("w1", "wp"):
                if (name, block) not in picked_codes:
                    held = work.tile([P, count * P], U32, name="slot_codes_" + name, align_bytes=64, bufs=AHEAD)
                    gather_into(picked_codes, name, held, x_codes, block, count)

        def first_layer(e, b):
            block = e * BLOCKS + b
            gather(block)
            acc = bank("a%d" % b, [P, H])
            for name in ("w1", "wp"):
                nc.tensor.matmul_mx(
                    out=acc[:],
                    lhsT=picked_codes[name, block].bitcast(FP8X4),
                    lhsT_scale=picked_plane[name, block],
                    rhs=codes[name, e].bitcast(FP8X4),
                    rhs_scale=first_scales(name, e),
                    start=(name == "w1"),
                    stop=(name == "wp"),
                )
            return acc

        def relu(acc, on_vector):
            pos = work.tile([P, PACK, P], F32, name="pos", bufs=2 * BLOCKS)
            src = acc[:].rearrange("s (m t) -> s t m", t=PACK)
            if on_vector:
                nc.vector.tensor_scalar_max(pos[:], src, 0.0)
            else:
                nc.scalar.activation(pos[:], src, ACT.Relu)
            return pos

        def turn(e, b, pos):
            turned = bank("%s%d" % ("pq"[b], e % (2 + b)), [P, PACK, P])
            for t in range(PACK):
                nc.tensor.transpose(turned[:, t, :], pos[:, t, :], ident[:])
            return turned

        def squares(e, turned):
            hidden[e] = keep.tile([P, C, PACK], BF16, name="hidden_%d" % e, align_bytes=64)
            for b in range(BLOCKS):
                src = turned[b][:].rearrange("m t s -> m s t")
                nc.scalar.activation(hidden[e][:, b * P : (b + 1) * P, :], src, ACT.Square)

        def quantise(e, slots):
            width = slots.stop - slots.start
            h_codes = work.tile([P, width], U32, name="h_codes", align_bytes=64)
            h_plane = work.tile([P, width], U8, name="h_plane", align_bytes=64)
            src = hidden[e][:, slots, :].rearrange("m s t -> m (s t)")
            nc.vector.quantize_mx(out=h_codes[:].bitcast(FP8X4), scales=h_plane[:], in_=src)
            return h_codes, h_plane

        def second_layer(e, slots, quantised, tag):
            h_codes, h_plane = quantised
            acc = bank(tag, [P, N // P, slots.stop - slots.start])
            for u in range(N // P):
                nc.tensor.matmul_mx(
                    out=acc[:, u, :],
                    lhsT=codes["w2", e][:, u * P : (u + 1) * P].bitcast(FP8X4),
                    lhsT_scale=w2_plane[W2_ROW:P, e * N + u * P : e * N + (u + 1) * P],
                    rhs=h_codes[:].bitcast(FP8X4),
                    rhs_scale=h_plane[:],
                    start=True,
                    stop=True,
                )
            return acc

        def leave(e, slots, acc):
            y = work.tile([P, N // P, slots.stop - slots.start], F32, name="y", bufs=LAST + BLOCKS)
            if e in VECTOR_OUT:
                nc.vector.tensor_copy(y[:], acc[:])
            else:
                nc.scalar.copy(y[:], acc[:])
            nc.sync.dma_start(out=out_rows[:, :, e * C + slots.start : e * C + slots.stop], in_=y[:])

        whole = slice(0, C)
        accs = [first_layer(0, b) for b in range(BLOCKS)]
        turned = None
        for e in range(E):
            behind = e - LAG
            if behind >= 0:
                quantised = quantise(behind, whole)
            if e < LAST:
                gather((e + 1) * BLOCKS)
            if behind >= 0:
                sums = second_layer(behind, whole, quantised, "q%d" % ((e + 1) % 3))
            if e == LAST:
                squares(e - 1, turned)
            rectified = [relu(accs[0], e == LAST)]
            if e < LAST:
                accs[0] = first_layer(e + 1, 0)
            rectified.append(relu(accs[1], False))
            if behind >= 0:
                leave(behind, whole, sums)
            before = turned
            turned = [turn(e, b, rectified[b]) for b in range(BLOCKS)]
            if e < LAST:
                accs[1] = first_layer(e + 1, 1)
                if e > 0:
                    squares(e - 1, before)

        for e, tag in zip(range(E - LAG, LAST), ("z", "q%d" % ((LAST - 2) % 3))):
            leave(e, whole, second_layer(e, whole, quantise(e, whole), tag))
        squares(LAST, turned)
        for b in range(BLOCKS):
            slots = slice(b * P, (b + 1) * P)
            leave(LAST, slots, second_layer(LAST, slots, quantise(LAST, slots), "a%d" % b))
